import numpy as np
import ml_dtypes


def mxq(x, axis, fmt="e4m3"):
    dtype, down = {"e4m3": (ml_dtypes.float8_e4m3fn, 7), "e5m2": (ml_dtypes.float8_e5m2, 14)}[fmt]
    v = np.moveaxis(np.asarray(x, np.float32).astype(ml_dtypes.bfloat16).astype(np.float64), axis, -1)
    blocks = v.reshape(v.shape[:-1] + (-1, 32))
    amax = np.abs(blocks).max(-1, keepdims=True)
    byte = np.maximum(np.where(amax > 0, np.frexp(amax)[1] - 1 + 127, 0) - down, 1)
    scale = np.exp2(byte - 127.0)
    codes = (blocks / scale).astype(np.float32).astype(dtype).astype(np.float64)
    return np.moveaxis((codes * scale).reshape(v.shape), -1, axis)


WIDE = False


def mx_kscale(k):
    if not WIDE:
        return np.ones(k)
    levels = np.array([10, -10, 5, -5, 0])
    if k % 512:
        return np.exp2(np.random.permutation(np.resize(levels, k // 32))).repeat(32)
    a = np.empty((k // 512, 16))
    for p in range(k // 512):
        a[p, :8] = np.random.permutation(np.resize(levels, 8))
        for g in range(8):
            far = levels[np.abs(levels - a[p, g]) >= 10]
            a[p, g + 8] = far[np.random.randint(len(far))]
    return np.exp2(a.ravel()).repeat(32)


def f64(x):
    return np.asarray(x).astype(np.float64)


def striped8(idx):
    return np.concatenate([x.reshape(-1, 16).T for x in idx]).astype(np.uint16)


def runs(offs, k):
    lists = np.stack([offs[16 * r : 16 * r + 16].T.reshape(-1) for r in range(8)]).astype(np.int64)
    return lists[np.arange(k) % 512 // 64]


def pack_weight(w):
    k, n = w.shape
    w = f64(np.asarray(w, np.float32).astype(ml_dtypes.bfloat16)).reshape(k // 32, 32, n)
    amax = np.abs(w).max(1)
    byte = np.clip(np.where(amax > 0, np.frexp(amax)[1] - 1 + 127 - 7, 1), 1, 254)
    scaled = (w * np.exp2(127.0 - byte)[:, None, :]).reshape(k, n).astype(np.float32)
    words = np.ascontiguousarray(scaled.reshape(k // 512, 128, 4, n).transpose(0, 1, 3, 2)).astype(ml_dtypes.float8_e4m3fn).view(np.uint8)
    return words, np.ascontiguousarray(byte.astype(np.uint8).reshape(k // 512, 16, n))


def unpack_weight(words, scales):
    g, p, n, _ = words.shape
    vals = np.ascontiguousarray(words).view(ml_dtypes.float8_e4m3fn).astype(np.float64) * np.repeat(np.exp2(scales.astype(np.float64) - 127.0), 8, axis=1)[..., None]
    return vals.transpose(0, 1, 3, 2).reshape(g * 512, n)


E2M1 = np.array([0.0, 0.5, 1.0, 1.5, 2.0, 3.0, 4.0, 6.0, -0.0, -0.5, -1.0, -1.5, -2.0, -3.0, -4.0, -6.0])


def pack_fp4(w):
    k, n = w.shape
    w = f64(np.asarray(w, np.float32).astype(ml_dtypes.bfloat16)).reshape(k // 32, 32, n)
    amax = np.abs(w).max(1)
    mant, ex = np.frexp(amax / 6.0)
    byte = np.clip(np.where(amax > 0, np.where(mant > 0.5, ex, ex - 1) + 127, 1), 1, 254)
    scaled = (w * np.exp2(127.0 - byte)[:, None, :]).reshape(k, n).astype(np.float32)
    c = np.ascontiguousarray(scaled.reshape(k // 512, 128, 4, n).transpose(0, 1, 3, 2)).astype(ml_dtypes.float4_e2m1fn).view(np.uint8) & 0xF
    words = (c[..., 0::2] | (c[..., 1::2] << 4)).reshape(k // 512, 128, 2 * n)
    return np.ascontiguousarray(words), np.ascontiguousarray(byte.astype(np.uint8).reshape(k // 512, 16, n))


def unpack_fp4(words, scales):
    g, _, n = scales.shape
    words = np.ascontiguousarray(words).reshape(g, 128, n, 2)
    nib = np.empty((g, 128, n, 4), np.uint8)
    nib[..., 0::2] = words & 0xF
    nib[..., 1::2] = words >> 4
    vals = E2M1[nib] * np.repeat(np.exp2(scales.astype(np.float64) - 127.0), 8, axis=1)[..., None]
    return vals.transpose(0, 1, 3, 2).reshape(g * 512, n)


def sigmoid(v):
    return 1.0 / (1.0 + np.exp(-np.maximum(v, -700.0)))

def planes(y):
    n, m = y.shape
    v = y.astype(np.float32).astype(ml_dtypes.bfloat16).astype(np.float64).reshape(n // 32, 32, m)
    top = np.abs(v).max(1)
    byte = np.clip(np.where(top > 0, np.frexp(top)[1] - 1 + 127 - 7, 1), 1, 254)
    codes = (v * np.exp2(127.0 - byte)[:, None, :]).reshape(n, m).astype(np.float32).astype(ml_dtypes.float8_e4m3fn).view(np.uint8)
    words = codes.reshape(n // 512, 128, 4, m).transpose(0, 1, 3, 2)
    return np.ascontiguousarray(words), np.ascontiguousarray(byte.astype(np.uint8).reshape(n // 512, 16, m))


K, T, S, N, H = 512, 2048, 512, 512, 512


def setup_inputs():
    n = np.random.standard_normal
    s = mx_kscale(K)[:, None]
    u = mx_kscale(H)
    packed_xT = pack_weight(n((K, T)) * s)
    packed_w1 = pack_fp4(n((K, H)) / np.sqrt(K) / s)
    packed_w2 = pack_fp4(n((H, N)) / np.sqrt(H) / u[:, None])
    return {
        "x_words": packed_xT[0],
        "x_scales": packed_xT[1],
        "w1_words": packed_w1[0],
        "w1_scales": packed_w1[1],
        "gn": (np.random.uniform(0.5, 1.5, (H, 1)) * u[:, None]).astype(np.float32),
        "w2_words": packed_w2[0],
        "w2_scales": packed_w2[1],
        "offs": striped8(np.random.randint(0, T, (8, S))),
        "n1": striped8(np.stack([np.random.permutation(S) for _ in range(8)])),
        "n2": striped8(np.stack([np.random.permutation(S) for _ in range(8)])),
        "n3": striped8(np.stack([np.random.permutation(S) for _ in range(8)])),
    }


def reference(x_words, x_scales, w1_words, w1_scales, gn, w2_words, w2_scales, offs, n1, n2, n3):
    xq = unpack_weight(x_words, x_scales)[np.arange(K)[:, None], runs(offs, K)]
    y = unpack_fp4(w1_words, w1_scales).T @ xq
    z = f64(gn) * (np.maximum(y, y[np.arange(H)[:, None], runs(n1, H)]))
    h = unpack_fp4(w2_words, w2_scales).T @ mxq(z, 0, "e4m3")
    out_0 = (h - (h[np.arange(N)[:, None], runs(n2, N)])) * (sigmoid(h[np.arange(N)[:, None], runs(n3, N)]))
    return (out_0,) + planes(out_0)

@@ -1,0 +1,195 @@
+from contextlib import ExitStack
+
+import concourse.mybir as mybir
+
+K, T, S, H, N = 512, 2048, 512, 512, 512
+FLOPS = 2 * K * H * S + 2 * H * N * S
+
+F32 = mybir.dt.float32
+BF16 = mybir.dt.bfloat16
+I32 = mybir.dt.int32
+U32 = mybir.dt.uint32
+U16 = mybir.dt.uint16
+U8 = mybir.dt.uint8
+FP8X4 = mybir.dt.float8_e4m3fn_x4
+FP4X4 = mybir.dt.float4_e2m1fn_x4
+ALU = mybir.AluOpType
+ACT = mybir.ActivationFunctionType
+
+P = 128
+PACK = 4
+HALF = S // 2
+
+
+def lists(tile, c0, width):
+    return tile[:, c0 // 16 : (c0 + width) // 16]
+
+
+def interleave(copy, dst, src):
+    copy(
+        out=dst.rearrange("p (c i t) -> p c t i", i=4, t=PACK),
+        in_=src.rearrange("p t (c i) -> p c t i", i=4),
+    )
+
+
+def tile_picked_hashbiggdif_none_po_kernel(
+    tc, x_words, x_scales, w1_words, w1_scales, gn, w2_words, w2_scales, offs, n1, n2, n3, out_0, out_1, out_2
+):
+    nc = tc.nc
+    with ExitStack() as ctx:
+        keep = ctx.enter_context(tc.tile_pool(name="keep", bufs=1))
+        psum = ctx.enter_context(tc.psum_pool(name="psum", bufs=1))
+
+        def sb(name, shape, dtype, tag=None):
+            return keep.tile(shape, dtype, name=name, tag=tag or name, align_bytes=64)
+
+        offs_t = sb("offs_t", [P, S // 16], U16)
+        n1_t = sb("n1_t", [P, S // 16], U16)
+        n2_t = sb("n2_t", [P, S // 16], U16)
+        n3_t = sb("n3_t", [P, S // 16], U16)
+        xw = sb("xw", [P, T], I32)
+        xs = sb("xs", [P, T], U8)
+        gw = sb("gw", [P, S], U32)
+        gs = sb("gs", [P, S], U8)
+        xplane = sb("xplane", [P, S], U8)
+        wraw = [sb("wraw%d" % i, [P, 2 * H], U8) for i in range(2)]
+        sraw = [sb("sraw0", [P, H], U8)]
+        wd = [sb("wd0", [P, 2 * H], U8)]
+        sd = [sb("sd0", [P, H], U8)]
+        gain = sb("gain", [P, PACK], F32)
+        warm = sb("warm", [P, 2], F32)
+
+        def load_plane(tile, scales):
+            for q in range(4):
+                nc.sync.dma_start(
+                    out=tile[32 * q : 32 * q + 32, :].bitcast(I32),
+                    in_=scales[0, 4 * q : 4 * q + 4, :].bitcast(I32).unsqueeze(0).broadcast_to([8, 4, H // 4]),
+                )
+
+        nc.gpsimd.memset(warm[:], 0.0)
+        nc.vector.memset(xplane[:].bitcast(I32), 0)
+
+        nc.scalar.dma_start(out=wraw[0][:].bitcast(I32), in_=w1_words[0].bitcast(I32))
+        nc.scalar.dma_start(out=xw[:], in_=x_words[0].rearrange("p c r -> p (c r)").bitcast(I32))
+        nc.sync.dma_start(offs_t[:], offs)
+        nc.sync.dma_start(
+            out=xs[:].bitcast(I32), in_=x_scales[0].bitcast(I32).unsqueeze(1).broadcast_to([16, 8, T // 4])
+        )
+        load_plane(sraw[0], w1_scales)
+        nc.sync.dma_start(n1_t[:], n1)
+        nc.sync.dma_start(n2_t[:], n2)
+        nc.sync.dma_start(n3_t[:], n3)
+        nc.sync.dma_start(out=wraw[1][:].bitcast(I32), in_=w2_words[0].bitcast(I32))
+        nc.gpsimd.dma_start(out=gain[:], in_=gn.rearrange("(p t) o -> p (t o)", t=PACK))
+        nc.scalar.activation(warm[:, 1:2], warm[:, 0:1], ACT.Sigmoid)
+
+        def deal_words(i):
+            nc.vector.tensor_copy(
+                out=wd[i][:].rearrange("p (t m b) -> p t m b", t=PACK, b=2),
+                in_=wraw[i][:].rearrange("p (m t b) -> p t m b", t=PACK, b=2),
+            )
+
+        def deal_scales(i):
+            nc.vector.tensor_copy(
+                out=sd[i][:].rearrange("p (t m) -> p t m", t=PACK),
+                in_=sraw[i][:].rearrange("p (m t) -> p t m", t=PACK),
+            )
+
+        def product(i, t, half, codes, plane):
+            bank = psum.tile([P, HALF], F32, name="bank", tag="bank%d" % (2 * t + half))
+            nc.tensor.matmul_mx(
+                out=bank[:],
+                lhsT=wd[i][:, 2 * P * t : 2 * P * (t + 1)].bitcast(FP4X4),
+                lhsT_scale=sd[i][:, P * t : P * (t + 1)],
+                rhs=codes.bitcast(FP8X4),
+                rhs_scale=plane,
+                start=True,
+                stop=True,
+            )
+            return bank
+
+        halves = [slice(0, HALF), slice(HALF, S)]
+
+        nc.vector.tensor_copy(gs[:], xs[:].indirect(offs_t[:]))
+        for q in range(4):
+            nc.scalar.dma_start(
+                out=xplane[32 * q : 32 * q + 4, :].bitcast(I32), in_=gs[32 * q : 32 * q + 32 : 8, :].bitcast(I32)
+            )
+        sraw.append(sb("sraw1", [P, H], U8, tag="xs"))
+        load_plane(sraw[1], w2_scales)
+        deal_words(0)
+        deal_scales(0)
+        for half in range(2):
+            nc.vector.tensor_copy(gw[:, halves[half]], xw[:].bitcast(U32).indirect(lists(offs_t, half * HALF, HALF)))
+        wd.append(sb("wd1", [P, 2 * H], U8, tag="xw"))
+        deal_words(1)
+
+        y = [sb("y%d" % t, [P, S], F32) for t in range(PACK)]
+        for t in range(PACK):
+            for half in range(2):
+                bank = product(0, t, half, gw[:, halves[half]], xplane[:, halves[half]])
+                nc.scalar.copy(out=y[t][:, halves[half]], in_=bank[:])
+        sd.append(sb("sd1", [P, H], U8, tag="gw"))
+        deal_scales(1)
+
+        hp = [sb("hp%d" % t, [P, S], F32) for t in range(PACK)]
+        hn = [sb("hn%d" % t, [P, S], F32) for t in range(PACK)]
+        for half in range(2):
+            cols = halves[half]
+            fetched = sb("fetched%d" % half, [P, PACK, HALF], F32)
+            larger = sb("larger%d" % half, [P, PACK, HALF], F32)
+            zrows = sb("zrows%d" % half, [P, PACK, HALF], BF16)
+            zk = sb("zk%d" % half, [P, PACK * HALF], BF16)
+            zw = sb("zw%d" % half, [P, HALF], U32)
+            zs = sb("zs%d" % half, [P, HALF], U8)
+
+            def finish(t):
+                nc.vector.tensor_tensor(larger[:, t, :], fetched[:, t, :], y[t][:, cols], ALU.max)
+                if half == 1 and t == PACK - 1:
+                    nc.vector.tensor_scalar(zrows[:, t, :], larger[:, t, :], gain[:, t : t + 1], None, ALU.mult)
+                else:
+                    nc.scalar.activation(zrows[:, t, :], larger[:, t, :], ACT.Copy, scale=gain[:, t : t + 1])
+
+            for t in range(PACK):
+                nc.vector.tensor_copy(fetched[:, t, :], y[t][:].indirect(lists(n1_t, half * HALF, HALF)))
+                if t > 0:
+                    finish(t - 1)
+            finish(PACK - 1)
+            interleave(nc.scalar.copy if half == 0 else nc.vector.tensor_copy, zk[:], zrows[:])
+            nc.vector.quantize_mx(out=zw[:].bitcast(FP8X4), scales=zs[:], in_=zk[:])
+            for t in range(PACK):
+                bank = product(1, t, half, zw[:], zs[:])
+                if half == 1 and t == 1:
+                    nc.vector.tensor_scalar(hn[t][:, cols], bank[:], -1.0, None, ALU.mult)
+                    nc.vector.tensor_copy(out=hp[t][:, cols], in_=bank[:])
+                else:
+                    nc.scalar.activation(hn[t][:, cols], bank[:], ACT.Copy, scale=-1.0)
+                    nc.scalar.copy(out=hp[t][:, cols], in_=bank[:])
+
+        out_rows = out_0.rearrange("(p t) c -> p t c", t=PACK)
+        out_words = out_1[0].rearrange("p c r -> p (c r)").bitcast(I32)
+        ow = sb("ow", [P, S], U32)
+        oplane = sb("oplane", [P, S], U8)
+        for half in range(2):
+            cols = halves[half]
+            diff = sb("diff%d" % half, [P, PACK, HALF], F32)
+            gate = sb("gate%d" % half, [P, PACK, HALF], F32)
+            res = sb("res%d" % half, [P, PACK, HALF], F32)
+            rk = sb("rk%d" % half, [P, PACK * HALF], BF16)
+            for t in range(PACK):
+                nc.vector.tensor_tensor(
+                    diff[:, t, :], hn[t][:].indirect(lists(n2_t, half * HALF, HALF)), hp[t][:, cols], ALU.add
+                )
+                nc.scalar.activation(gate[:, t, :], hp[t][:].indirect(lists(n3_t, half * HALF, HALF)), ACT.Sigmoid)
+                if t % 2 == 1:
+                    pair = slice(t - 1, t + 1)
+                    nc.vector.tensor_tensor(res[:, pair, :], diff[:, pair, :], gate[:, pair, :], ALU.mult)
+                    nc.sync.dma_start(out=out_rows[:, pair, cols], in_=res[:, pair, :])
+            interleave(nc.scalar.copy if half == 0 else nc.vector.tensor_copy, rk[:], res[:])
+            nc.vector.quantize_mx(out=ow[:, cols].bitcast(FP8X4), scales=oplane[:, cols], in_=rk[:])
+            nc.sync.dma_start(out=out_words[:, cols], in_=ow[:, cols].bitcast(I32))
+        for q in range(4):
+            queue = nc.scalar if q % 2 == 0 else nc.sync
+            queue.dma_start(
+                out=out_2[0, 4 * q : 4 * q + 4, :].bitcast(I32), in_=oplane[32 * q : 32 * q + 4, :].bitcast(I32)
+            )

@@ -59,6 +59,7 @@ def tile_picked_hashbiggdif_none_po_kernel(
         gain = sb("gain", [P, PACK], F32)
         warm = sb("warm", [P, 2], F32)
 
+
         def load_plane(tile, scales):
             for q in range(4):
                 nc.sync.dma_start(
@@ -69,17 +70,17 @@ def tile_picked_hashbiggdif_none_po_kernel(
         nc.gpsimd.memset(warm[:], 0.0)
         nc.vector.memset(xplane[:].bitcast(I32), 0)
 
-        nc.scalar.dma_start(out=wraw[0][:].bitcast(I32), in_=w1_words[0].bitcast(I32))
-        nc.scalar.dma_start(out=xw[:], in_=x_words[0].rearrange("p c r -> p (c r)").bitcast(I32))
-        nc.sync.dma_start(offs_t[:], offs)
-        nc.sync.dma_start(
+        nc.scalar.dma_start(
             out=xs[:].bitcast(I32), in_=x_scales[0].bitcast(I32).unsqueeze(1).broadcast_to([16, 8, T // 4])
         )
+        nc.scalar.dma_start(out=xw[:], in_=x_words[0].rearrange("p c r -> p (c r)").bitcast(I32))
+        nc.sync.dma_start(offs_t[:], offs)
+        nc.sync.dma_start(out=wraw[0][:].bitcast(I32), in_=w1_words[0].bitcast(I32))
         load_plane(sraw[0], w1_scales)
+        nc.sync.dma_start(out=wraw[1][:].bitcast(I32), in_=w2_words[0].bitcast(I32))
         nc.sync.dma_start(n1_t[:], n1)
         nc.sync.dma_start(n2_t[:], n2)
         nc.sync.dma_start(n3_t[:], n3)
-        nc.sync.dma_start(out=wraw[1][:].bitcast(I32), in_=w2_words[0].bitcast(I32))
         nc.gpsimd.dma_start(out=gain[:], in_=gn.rearrange("(p t) o -> p (t o)", t=PACK))
         nc.scalar.activation(warm[:, 1:2], warm[:, 0:1], ACT.Sigmoid)
 
@@ -95,10 +96,9 @@ def tile_picked_hashbiggdif_none_po_kernel(
                 in_=sraw[i][:].rearrange("p (m t) -> p t m", t=PACK),
             )
 
-        def product(i, t, half, codes, plane):
-            bank = psum.tile([P, HALF], F32, name="bank", tag="bank%d" % (2 * t + half))
+        def product(i, t, out, codes, plane):
             nc.tensor.matmul_mx(
-                out=bank[:],
+                out=out,
                 lhsT=wd[i][:, 2 * P * t : 2 * P * (t + 1)].bitcast(FP4X4),
                 lhsT_scale=sd[i][:, P * t : P * (t + 1)],
                 rhs=codes.bitcast(FP8X4),
@@ -106,7 +106,6 @@ def tile_picked_hashbiggdif_none_po_kernel(
                 start=True,
                 stop=True,
             )
-            return bank
 
         halves = [slice(0, HALF), slice(HALF, S)]
 
@@ -119,75 +118,144 @@ def tile_picked_hashbiggdif_none_po_kernel(
         load_plane(sraw[1], w2_scales)
         deal_words(0)
         deal_scales(0)
-        for half in range(2):
-            nc.vector.tensor_copy(gw[:, halves[half]], xw[:].bitcast(U32).indirect(lists(offs_t, half * HALF, HALF)))
+        nc.vector.tensor_copy(gw[:], xw[:].bitcast(U32).indirect(offs_t[:]))
         wd.append(sb("wd1", [P, 2 * H], U8, tag="xw"))
         deal_words(1)
 
         y = [sb("y%d" % t, [P, S], F32) for t in range(PACK)]
+        ybank = [psum.tile([P, S], F32, name="ybank", tag="bank%d" % b) for b in range(PACK + 1)]
         for t in range(PACK):
             for half in range(2):
-                bank = product(0, t, half, gw[:, halves[half]], xplane[:, halves[half]])
-                nc.scalar.copy(out=y[t][:, halves[half]], in_=bank[:])
+                place = ybank[t + 1 - half][:, halves[half]]
+                product(0, t, place, gw[:, halves[half]], xplane[:, halves[half]])
+                nc.scalar.copy(out=y[t][:, halves[half]], in_=place)
         sd.append(sb("sd1", [P, H], U8, tag="gw"))
         deal_scales(1)
 
-        hp = [sb("hp%d" % t, [P, S], F32) for t in range(PACK)]
-        hn = [sb("hn%d" % t, [P, S], F32) for t in range(PACK)]
-        for half in range(2):
+        h = [sb("h%d" % t, [P, S], F32) for t in range(PACK)]
+        hplain = [sb("hplain%d" % half, [P, PACK, HALF], F32) for half in range(2)]
+        zrows = [sb("zrows0", [P, PACK, HALF], BF16, tag="xplane"), sb("zrows1", [P, PACK, HALF], BF16)]
+        zk = [sb("zk%d" % half, [P, PACK * HALF], BF16) for half in range(2)]
+        zw = [sb("zw%d" % half, [P, HALF], U32) for half in range(2)]
+        zs = [sb("zs%d" % half, [P, HALF], U8) for half in range(2)]
+        fetched = {}
+        larger = {}
+        hbank = {}
+
+        def neighbours(half, t, tag=None):
+            fetched[half, t] = sb("fetched%d%d" % (half, t), [P, HALF], F32, tag=tag)
+            nc.vector.tensor_copy(fetched[half, t][:], y[t][:].indirect(lists(n1_t, half * HALF, HALF)))
+
+        def take_larger(half, t, tag=None):
+            larger[half, t] = sb("larger%d%d" % (half, t), [P, HALF], F32, tag=tag)
+            own = ybank[t + 1][:, halves[0]] if half == 0 else y[t][:, halves[1]]
+            nc.vector.tensor_tensor(larger[half, t][:], fetched[half, t][:], own, ALU.max)
+
+        def gain_on_scalar(half, t):
+            nc.scalar.activation(zrows[half][:, t, :], larger[half, t][:], ACT.Copy, scale=gain[:, t : t + 1])
+
+        def gain_on_vector(half, t):
+            nc.vector.tensor_scalar(zrows[half][:, t, :], larger[half, t][:], gain[:, t : t + 1], None, ALU.mult)
+
+        def quantise_z(half):
+            nc.vector.quantize_mx(out=zw[half][:].bitcast(FP8X4), scales=zs[half][:], in_=zk[half][:])
+
+        def second_product(half, tags):
             cols = halves[half]
-            fetched = sb("fetched%d" % half, [P, PACK, HALF], F32)
-            larger = sb("larger%d" % half, [P, PACK, HALF], F32)
-            zrows = sb("zrows%d" % half, [P, PACK, HALF], BF16)
-            zk = sb("zk%d" % half, [P, PACK * HALF], BF16)
-            zw = sb("zw%d" % half, [P, HALF], U32)
-            zs = sb("zs%d" % half, [P, HALF], U8)
-
-            def finish(t):
-                nc.vector.tensor_tensor(larger[:, t, :], fetched[:, t, :], y[t][:, cols], ALU.max)
-                if half == 1 and t == PACK - 1:
-                    nc.vector.tensor_scalar(zrows[:, t, :], larger[:, t, :], gain[:, t : t + 1], None, ALU.mult)
-                else:
-                    nc.scalar.activation(zrows[:, t, :], larger[:, t, :], ACT.Copy, scale=gain[:, t : t + 1])
-
             for t in range(PACK):
-                nc.vector.tensor_copy(fetched[:, t, :], y[t][:].indirect(lists(n1_t, half * HALF, HALF)))
-                if t > 0:
-                    finish(t - 1)
-            finish(PACK - 1)
-            interleave(nc.scalar.copy if half == 0 else nc.vector.tensor_copy, zk[:], zrows[:])
-            nc.vector.quantize_mx(out=zw[:].bitcast(FP8X4), scales=zs[:], in_=zk[:])
-            for t in range(PACK):
-                bank = product(1, t, half, zw[:], zs[:])
-                if half == 1 and t == 1:
-                    nc.vector.tensor_scalar(hn[t][:, cols], bank[:], -1.0, None, ALU.mult)
-                    nc.vector.tensor_copy(out=hp[t][:, cols], in_=bank[:])
-                else:
-                    nc.scalar.activation(hn[t][:, cols], bank[:], ACT.Copy, scale=-1.0)
-                    nc.scalar.copy(out=hp[t][:, cols], in_=bank[:])
+                bank = psum.tile([P, HALF], F32, name="hbank", tag=tags[t])
+                product(1, t, bank[:], zw[half][:], zs[half][:])
+                nc.scalar.copy(out=h[t][:, cols], in_=bank[:])
+                hbank[half, t] = bank
+                if half == 0:
+                    nc.scalar.copy(out=hplain[half][:, t, :], in_=bank[:])
+
+        neighbours(0, 0)
+        for t in range(1, PACK):
+            neighbours(0, t)
+            take_larger(0, t - 1)
+            gain_on_scalar(0, t - 1)
+        neighbours(1, 0, tag="larger01")
+        take_larger(0, 3)
+        gain_on_scalar(0, 3)
+        interleave(nc.scalar.copy, zk[0][:], zrows[0][:])
+        neighbours(1, 1, tag="larger02")
+        take_larger(1, 0)
+        gain_on_scalar(1, 0)
+        neighbours(1, 2, tag="larger03")
+        take_larger(1, 1)
+        gain_on_scalar(1, 1)
+        quantise_z(0)
+        second_product(0, ["bank5", "bank6", "bank7", "bank0"])
+        neighbours(1, 3, tag="xplane")
+        take_larger(1, 2, tag="zk0")
+        take_larger(1, 3)
+        gain_on_vector(1, 2)
+        gain_on_vector(1, 3)
+        for part in range(2):
+            interleave(
+                nc.vector.tensor_copy,
+                zk[1][:, part * 2 * HALF : (part + 1) * 2 * HALF],
+                zrows[1][:, :, part * P : (part + 1) * P],
+            )
+        for part in range(2):
+            cols = slice(part * P, (part + 1) * P)
+            nc.vector.quantize_mx(
+                out=zw[1][:, cols].bitcast(FP8X4),
+                scales=zs[1][:, cols],
+                in_=zk[1][:, part * 2 * HALF : (part + 1) * 2 * HALF],
+            )
+        second_product(1, ["bank1", "bank2", "bank3", "bank4"])
 
         out_rows = out_0.rearrange("(p t) c -> p t c", t=PACK)
         out_words = out_1[0].rearrange("p c r -> p (c r)").bitcast(I32)
         ow = sb("ow", [P, S], U32)
         oplane = sb("oplane", [P, S], U8)
-        for half in range(2):
+        diff = [sb("diff%d" % half, [P, PACK, HALF], F32, tag=None) for half in range(2)]
+        gate = [sb("gate%d" % half, [P, PACK, HALF], F32, tag=["zw1", "zs1"][half]) for half in range(2)]
+        res = [sb("res%d" % half, [P, PACK, HALF], F32) for half in range(2)]
+        rk = [sb("rk%d" % half, [P, PACK * HALF], BF16, tag=None) for half in range(2)]
+
+        def fetch(half, t):
+            nc.vector.tensor_tensor(
+                diff[half][:, t, :], h[t][:].indirect(lists(n2_t, half * HALF, HALF)), hplain[half][:, t, :], ALU.subtract
+            )
+            nc.scalar.activation(gate[half][:, t, :], h[t][:].indirect(lists(n3_t, half * HALF, HALF)), ACT.Sigmoid)
+
+        def combine(half, rows):
+            nc.vector.scalar_tensor_tensor(
+                res[half][:, rows, :], diff[half][:, rows, :], -1.0, gate[half][:, rows, :], ALU.mult, ALU.mult
+            )
+            nc.sync.dma_start(out=out_rows[:, rows, halves[half]], in_=res[half][:, rows, :])
+
+        def hand_on(half):
             cols = halves[half]
-            diff = sb("diff%d" % half, [P, PACK, HALF], F32)
-            gate = sb("gate%d" % half, [P, PACK, HALF], F32)
-            res = sb("res%d" % half, [P, PACK, HALF], F32)
-            rk = sb("rk%d" % half, [P, PACK * HALF], BF16)
-            for t in range(PACK):
-                nc.vector.tensor_tensor(
-                    diff[:, t, :], hn[t][:].indirect(lists(n2_t, half * HALF, HALF)), hp[t][:, cols], ALU.add
-                )
-                nc.scalar.activation(gate[:, t, :], hp[t][:].indirect(lists(n3_t, half * HALF, HALF)), ACT.Sigmoid)
-                if t % 2 == 1:
-                    pair = slice(t - 1, t + 1)
-                    nc.vector.tensor_tensor(res[:, pair, :], diff[:, pair, :], gate[:, pair, :], ALU.mult)
-                    nc.sync.dma_start(out=out_rows[:, pair, cols], in_=res[:, pair, :])
-            interleave(nc.scalar.copy if half == 0 else nc.vector.tensor_copy, rk[:], res[:])
-            nc.vector.quantize_mx(out=ow[:, cols].bitcast(FP8X4), scales=oplane[:, cols], in_=rk[:])
+            nc.vector.quantize_mx(out=ow[:, cols].bitcast(FP8X4), scales=oplane[:, cols], in_=rk[half][:])
             nc.sync.dma_start(out=out_words[:, cols], in_=ow[:, cols].bitcast(I32))
+
+        def second_copy(copy, t):
+            copy(out=hplain[1][:, t, :], in_=hbank[1, t][:])
+
+        second_copy(nc.vector.tensor_copy, 0)
+        fetch(0, 0)
+        fetch(0, 1)
+        second_copy(nc.scalar.copy, 1)
+        fetch(0, 2)
+        fetch(0, 3)
+        second_copy(nc.scalar.copy, 2)
+        second_copy(nc.scalar.copy, 3)
+        fetch(1, 0)
+        combine(0, slice(0, 2))
+        fetch(1, 1)
+        combine(0, slice(2, 4))
+        fetch(1, 2)
+        fetch(1, 3)
+        interleave(nc.scalar.copy, rk[0][:], res[0][:])
+        combine(1, slice(0, 2))
+        combine(1, slice(2, 4))
+        interleave(nc.vector.tensor_copy, rk[1][:], res[1][:])
+        hand_on(0)
+        hand_on(1)
         for q in range(4):
             queue = nc.scalar if q % 2 == 0 else nc.sync
             queue.dma_start(

@@ -60,9 +60,9 @@ def tile_picked_hashbiggdif_none_po_kernel(
         warm = sb("warm", [P, 2], F32)
 
 
-        def load_plane(tile, scales):
-            for q in range(4):
-                nc.sync.dma_start(
+        def load_plane(tile, scales, quadrants, queue):
+            for q in quadrants:
+                queue.dma_start(
                     out=tile[32 * q : 32 * q + 32, :].bitcast(I32),
                     in_=scales[0, 4 * q : 4 * q + 4, :].bitcast(I32).unsqueeze(0).broadcast_to([8, 4, H // 4]),
                 )
@@ -73,14 +73,15 @@ def tile_picked_hashbiggdif_none_po_kernel(
         nc.scalar.dma_start(
             out=xs[:].bitcast(I32), in_=x_scales[0].bitcast(I32).unsqueeze(1).broadcast_to([16, 8, T // 4])
         )
+        load_plane(sraw[0][:], w1_scales, (0, 1), nc.scalar)
         nc.scalar.dma_start(out=xw[:], in_=x_words[0].rearrange("p c r -> p (c r)").bitcast(I32))
         nc.sync.dma_start(offs_t[:], offs)
         nc.sync.dma_start(out=wraw[0][:].bitcast(I32), in_=w1_words[0].bitcast(I32))
-        load_plane(sraw[0], w1_scales)
-        nc.sync.dma_start(out=wraw[1][:].bitcast(I32), in_=w2_words[0].bitcast(I32))
+        load_plane(sraw[0][:], w1_scales, (2, 3), nc.sync)
         nc.sync.dma_start(n1_t[:], n1)
         nc.sync.dma_start(n2_t[:], n2)
         nc.sync.dma_start(n3_t[:], n3)
+        nc.gpsimd.dma_start(out=wraw[1][:].bitcast(I32), in_=w2_words[0].bitcast(I32))
         nc.gpsimd.dma_start(out=gain[:], in_=gn.rearrange("(p t) o -> p (t o)", t=PACK))
         nc.scalar.activation(warm[:, 1:2], warm[:, 0:1], ACT.Sigmoid)
 
@@ -111,11 +112,12 @@ def tile_picked_hashbiggdif_none_po_kernel(
 
         nc.vector.tensor_copy(gs[:], xs[:].indirect(offs_t[:]))
         for q in range(4):
-            nc.scalar.dma_start(
+            queue = nc.scalar if q % 2 == 0 else nc.sync
+            queue.dma_start(
                 out=xplane[32 * q : 32 * q + 4, :].bitcast(I32), in_=gs[32 * q : 32 * q + 32 : 8, :].bitcast(I32)
             )
         sraw.append(sb("sraw1", [P, H], U8, tag="xs"))
-        load_plane(sraw[1], w2_scales)
+        load_plane(sraw[1][:], w2_scales, range(4), nc.sync)
         deal_words(0)
         deal_scales(0)
         nc.vector.tensor_copy(gw[:], xw[:].bitcast(U32).indirect(offs_t[:]))

from contextlib import ExitStack

import concourse.mybir as mybir

K, T, S, H, N = 512, 2048, 512, 512, 512
FLOPS = 2 * K * H * S + 2 * H * N * S

F32 = mybir.dt.float32
BF16 = mybir.dt.bfloat16
I32 = mybir.dt.int32
U32 = mybir.dt.uint32
U16 = mybir.dt.uint16
U8 = mybir.dt.uint8
FP8X4 = mybir.dt.float8_e4m3fn_x4
FP4X4 = mybir.dt.float4_e2m1fn_x4
ALU = mybir.AluOpType
ACT = mybir.ActivationFunctionType

P = 128
PACK = 4
HALF = S // 2


def lists(tile, c0, width):
    return tile[:, c0 // 16 : (c0 + width) // 16]


def interleave(copy, dst, src):
    copy(
        out=dst.rearrange("p (c i t) -> p c t i", i=4, t=PACK),
        in_=src.rearrange("p t (c i) -> p c t i", i=4),
    )


def tile_picked_hashbiggdif_none_po_kernel(
    tc, x_words, x_scales, w1_words, w1_scales, gn, w2_words, w2_scales, offs, n1, n2, n3, out_0, out_1, out_2
):
    nc = tc.nc
    with ExitStack() as ctx:
        keep = ctx.enter_context(tc.tile_pool(name="keep", bufs=1))
        psum = ctx.enter_context(tc.psum_pool(name="psum", bufs=1))

        def sb(name, shape, dtype, tag=None):
            return keep.tile(shape, dtype, name=name, tag=tag or name, align_bytes=64)

        offs_t = sb("offs_t", [P, S // 16], U16)
        n1_t = sb("n1_t", [P, S // 16], U16)
        n2_t = sb("n2_t", [P, S // 16], U16)
        n3_t = sb("n3_t", [P, S // 16], U16)
        xw = sb("xw", [P, T], I32)
        xs = sb("xs", [P, T], U8)
        gw = sb("gw", [P, S], U32)
        gs = sb("gs", [P, S], U8)
        xplane = sb("xplane", [P, S], U8)
        wraw = [sb("wraw%d" % i, [P, 2 * H], U8) for i in range(2)]
        sraw = [sb("sraw0", [P, H], U8)]
        wd = [sb("wd0", [P, 2 * H], U8)]
        sd = [sb("sd0", [P, H], U8)]
        gain = sb("gain", [P, PACK], F32)
        warm = sb("warm", [P, 2], F32)


        def load_plane(tile, scales, quadrants, queue):
            for q in quadrants:
                queue.dma_start(
                    out=tile[32 * q : 32 * q + 32, :].bitcast(I32),
                    in_=scales[0, 4 * q : 4 * q + 4, :].bitcast(I32).unsqueeze(0).broadcast_to([8, 4, H // 4]),
                )

        nc.gpsimd.memset(warm[:], 0.0)
        nc.vector.memset(xplane[:].bitcast(I32), 0)

        nc.scalar.dma_start(
            out=xs[:].bitcast(I32), in_=x_scales[0].bitcast(I32).unsqueeze(1).broadcast_to([16, 8, T // 4])
        )
        load_plane(sraw[0][:], w1_scales, (0, 1), nc.scalar)
        nc.scalar.dma_start(out=xw[:], in_=x_words[0].rearrange("p c r -> p (c r)").bitcast(I32))
        nc.sync.dma_start(offs_t[:], offs)
        nc.sync.dma_start(out=wraw[0][:].bitcast(I32), in_=w1_words[0].bitcast(I32))
        load_plane(sraw[0][:], w1_scales, (2, 3), nc.sync)
        nc.sync.dma_start(n1_t[:], n1)
        nc.sync.dma_start(n2_t[:], n2)
        nc.sync.dma_start(n3_t[:], n3)
        nc.gpsimd.dma_start(out=wraw[1][:].bitcast(I32), in_=w2_words[0].bitcast(I32))
        nc.gpsimd.dma_start(out=gain[:], in_=gn.rearrange("(p t) o -> p (t o)", t=PACK))
        nc.scalar.activation(warm[:, 1:2], warm[:, 0:1], ACT.Sigmoid)

        def deal_words(i):
            nc.vector.tensor_copy(
                out=wd[i][:].rearrange("p (t m b) -> p t m b", t=PACK, b=2),
                in_=wraw[i][:].rearrange("p (m t b) -> p t m b", t=PACK, b=2),
            )

        def deal_scales(i):
            nc.vector.tensor_copy(
                out=sd[i][:].rearrange("p (t m) -> p t m", t=PACK),
                in_=sraw[i][:].rearrange("p (m t) -> p t m", t=PACK),
            )

        def product(i, t, out, codes, plane):
            nc.tensor.matmul_mx(
                out=out,
                lhsT=wd[i][:, 2 * P * t : 2 * P * (t + 1)].bitcast(FP4X4),
                lhsT_scale=sd[i][:, P * t : P * (t + 1)],
                rhs=codes.bitcast(FP8X4),
                rhs_scale=plane,
                start=True,
                stop=True,
            )

        halves = [slice(0, HALF), slice(HALF, S)]

        nc.vector.tensor_copy(gs[:], xs[:].indirect(offs_t[:]))
        for q in range(4):
            queue = nc.scalar if q % 2 == 0 else nc.sync
            queue.dma_start(
                out=xplane[32 * q : 32 * q + 4, :].bitcast(I32), in_=gs[32 * q : 32 * q + 32 : 8, :].bitcast(I32)
            )
        sraw.append(sb("sraw1", [P, H], U8, tag="xs"))
        load_plane(sraw[1][:], w2_scales, range(4), nc.sync)
        deal_words(0)
        deal_scales(0)
        nc.vector.tensor_copy(gw[:], xw[:].bitcast(U32).indirect(offs_t[:]))
        wd.append(sb("wd1", [P, 2 * H], U8, tag="xw"))
        deal_words(1)

        y = [sb("y%d" % t, [P, S], F32) for t in range(PACK)]
        ybank = [psum.tile([P, S], F32, name="ybank", tag="bank%d" % b) for b in range(PACK + 1)]
        for t in range(PACK):
            for half in range(2):
                place = ybank[t + 1 - half][:, halves[half]]
                product(0, t, place, gw[:, halves[half]], xplane[:, halves[half]])
                nc.scalar.copy(out=y[t][:, halves[half]], in_=place)
        sd.append(sb("sd1", [P, H], U8, tag="gw"))
        deal_scales(1)

        h = [sb("h%d" % t, [P, S], F32) for t in range(PACK)]
        hplain = [sb("hplain%d" % half, [P, PACK, HALF], F32) for half in range(2)]
        zrows = [sb("zrows0", [P, PACK, HALF], BF16, tag="xplane"), sb("zrows1", [P, PACK, HALF], BF16)]
        zk = [sb("zk%d" % half, [P, PACK * HALF], BF16) for half in range(2)]
        zw = [sb("zw%d" % half, [P, HALF], U32) for half in range(2)]
        zs = [sb("zs%d" % half, [P, HALF], U8) for half in range(2)]
        fetched = {}
        larger = {}
        hbank = {}

        def neighbours(half, t, tag=None):
            fetched[half, t] = sb("fetched%d%d" % (half, t), [P, HALF], F32, tag=tag)
            nc.vector.tensor_copy(fetched[half, t][:], y[t][:].indirect(lists(n1_t, half * HALF, HALF)))

        def take_larger(half, t, tag=None):
            larger[half, t] = sb("larger%d%d" % (half, t), [P, HALF], F32, tag=tag)
            own = ybank[t + 1][:, halves[0]] if half == 0 else y[t][:, halves[1]]
            nc.vector.tensor_tensor(larger[half, t][:], fetched[half, t][:], own, ALU.max)

        def gain_on_scalar(half, t):
            nc.scalar.activation(zrows[half][:, t, :], larger[half, t][:], ACT.Copy, scale=gain[:, t : t + 1])

        def gain_on_vector(half, t):
            nc.vector.tensor_scalar(zrows[half][:, t, :], larger[half, t][:], gain[:, t : t + 1], None, ALU.mult)

        def quantise_z(half):
            nc.vector.quantize_mx(out=zw[half][:].bitcast(FP8X4), scales=zs[half][:], in_=zk[half][:])

        def second_product(half, tags):
            cols = halves[half]
            for t in range(PACK):
                bank = psum.tile([P, HALF], F32, name="hbank", tag=tags[t])
                product(1, t, bank[:], zw[half][:], zs[half][:])
                nc.scalar.copy(out=h[t][:, cols], in_=bank[:])
                hbank[half, t] = bank
                if half == 0:
                    nc.scalar.copy(out=hplain[half][:, t, :], in_=bank[:])

        neighbours(0, 0)
        for t in range(1, PACK):
            neighbours(0, t)
            take_larger(0, t - 1)
            gain_on_scalar(0, t - 1)
        neighbours(1, 0, tag="larger01")
        take_larger(0, 3)
        gain_on_scalar(0, 3)
        interleave(nc.scalar.copy, zk[0][:], zrows[0][:])
        neighbours(1, 1, tag="larger02")
        take_larger(1, 0)
        gain_on_scalar(1, 0)
        neighbours(1, 2, tag="larger03")
        take_larger(1, 1)
        gain_on_scalar(1, 1)
        quantise_z(0)
        second_product(0, ["bank5", "bank6", "bank7", "bank0"])
        neighbours(1, 3, tag="xplane")
        take_larger(1, 2, tag="zk0")
        take_larger(1, 3)
        gain_on_vector(1, 2)
        gain_on_vector(1, 3)
        for part in range(2):
            interleave(
                nc.vector.tensor_copy,
                zk[1][:, part * 2 * HALF : (part + 1) * 2 * HALF],
                zrows[1][:, :, part * P : (part + 1) * P],
            )
        for part in range(2):
            cols = slice(part * P, (part + 1) * P)
            nc.vector.quantize_mx(
                out=zw[1][:, cols].bitcast(FP8X4),
                scales=zs[1][:, cols],
                in_=zk[1][:, part * 2 * HALF : (part + 1) * 2 * HALF],
            )
        second_product(1, ["bank1", "bank2", "bank3", "bank4"])

        out_rows = out_0.rearrange("(p t) c -> p t c", t=PACK)
        out_words = out_1[0].rearrange("p c r -> p (c r)").bitcast(I32)
        ow = sb("ow", [P, S], U32)
        oplane = sb("oplane", [P, S], U8)
        diff = [sb("diff%d" % half, [P, PACK, HALF], F32, tag=None) for half in range(2)]
        gate = [sb("gate%d" % half, [P, PACK, HALF], F32, tag=["zw1", "zs1"][half]) for half in range(2)]
        res = [sb("res%d" % half, [P, PACK, HALF], F32) for half in range(2)]
        rk = [sb("rk%d" % half, [P, PACK * HALF], BF16, tag=None) for half in range(2)]

        def fetch(half, t):
            nc.vector.tensor_tensor(
                diff[half][:, t, :], h[t][:].indirect(lists(n2_t, half * HALF, HALF)), hplain[half][:, t, :], ALU.subtract
            )
            nc.scalar.activation(gate[half][:, t, :], h[t][:].indirect(lists(n3_t, half * HALF, HALF)), ACT.Sigmoid)

        def combine(half, rows):
            nc.vector.scalar_tensor_tensor(
                res[half][:, rows, :], diff[half][:, rows, :], -1.0, gate[half][:, rows, :], ALU.mult, ALU.mult
            )
            nc.sync.dma_start(out=out_rows[:, rows, halves[half]], in_=res[half][:, rows, :])

        def hand_on(half):
            cols = halves[half]
            nc.vector.quantize_mx(out=ow[:, cols].bitcast(FP8X4), scales=oplane[:, cols], in_=rk[half][:])
            nc.sync.dma_start(out=out_words[:, cols], in_=ow[:, cols].bitcast(I32))

        def second_copy(copy, t):
            copy(out=hplain[1][:, t, :], in_=hbank[1, t][:])

        second_copy(nc.vector.tensor_copy, 0)
        fetch(0, 0)
        fetch(0, 1)
        second_copy(nc.scalar.copy, 1)
        fetch(0, 2)
        fetch(0, 3)
        second_copy(nc.scalar.copy, 2)
        second_copy(nc.scalar.copy, 3)
        fetch(1, 0)
        combine(0, slice(0, 2))
        fetch(1, 1)
        combine(0, slice(2, 4))
        fetch(1, 2)
        fetch(1, 3)
        interleave(nc.scalar.copy, rk[0][:], res[0][:])
        combine(1, slice(0, 2))
        combine(1, slice(2, 4))
        interleave(nc.vector.tensor_copy, rk[1][:], res[1][:])
        hand_on(0)
        hand_on(1)
        for q in range(4):
            queue = nc.scalar if q % 2 == 0 else nc.sync
            queue.dma_start(
                out=out_2[0, 4 * q : 4 * q + 4, :].bitcast(I32), in_=oplane[32 * q : 32 * q + 4, :].bitcast(I32)
            )
